import numpy as np
import ml_dtypes


def mxq(x, axis, fmt="e4m3"):
    dtype, down = {"e4m3": (ml_dtypes.float8_e4m3fn, 7), "e5m2": (ml_dtypes.float8_e5m2, 14)}[fmt]
    v = np.moveaxis(np.asarray(x, np.float32).astype(ml_dtypes.bfloat16).astype(np.float64), axis, -1)
    blocks = v.reshape(v.shape[:-1] + (-1, 32))
    amax = np.abs(blocks).max(-1, keepdims=True)
    byte = np.maximum(np.where(amax > 0, np.frexp(amax)[1] - 1 + 127, 0) - down, 1)
    scale = np.exp2(byte - 127.0)
    codes = (blocks / scale).astype(np.float32).astype(dtype).astype(np.float64)
    return np.moveaxis((codes * scale).reshape(v.shape), -1, axis)


WIDE = False


def mx_kscale(k):
    if not WIDE:
        return np.ones(k)
    levels = np.array([10, -10, 5, -5, 0])
    if k % 512:
        return np.exp2(np.random.permutation(np.resize(levels, k // 32))).repeat(32)
    a = np.empty((k // 512, 16))
    for p in range(k // 512):
        a[p, :8] = np.random.permutation(np.resize(levels, 8))
        for g in range(8):
            far = levels[np.abs(levels - a[p, g]) >= 10]
            a[p, g + 8] = far[np.random.randint(len(far))]
    return np.exp2(a.ravel()).repeat(32)


def f64(x):
    return np.asarray(x).astype(np.float64)


def striped(idx):
    return np.tile(idx.reshape(-1, 16).T, (8, 1)).astype(np.uint16)


def unstriped(offs):
    return offs[:16].T.reshape(-1).astype(np.int64)


E2M1 = np.array([0.0, 0.5, 1.0, 1.5, 2.0, 3.0, 4.0, 6.0, -0.0, -0.5, -1.0, -1.5, -2.0, -3.0, -4.0, -6.0])


def pack_fp4(w):
    k, n = w.shape
    w = f64(np.asarray(w, np.float32).astype(ml_dtypes.bfloat16)).reshape(k // 32, 32, n)
    amax = np.abs(w).max(1)
    mant, ex = np.frexp(amax / 6.0)
    byte = np.clip(np.where(amax > 0, np.where(mant > 0.5, ex, ex - 1) + 127, 1), 1, 254)
    scaled = (w * np.exp2(127.0 - byte)[:, None, :]).reshape(k, n).astype(np.float32)
    c = np.ascontiguousarray(scaled.reshape(k // 512, 128, 4, n).transpose(0, 1, 3, 2)).astype(ml_dtypes.float4_e2m1fn).view(np.uint8) & 0xF
    words = (c[..., 0::2] | (c[..., 1::2] << 4)).reshape(k // 512, 128, 2 * n)
    return np.ascontiguousarray(words), np.ascontiguousarray(byte.astype(np.uint8).reshape(k // 512, 16, n))


def unpack_fp4(words, scales):
    g, _, n = scales.shape
    words = np.ascontiguousarray(words).reshape(g, 128, n, 2)
    nib = np.empty((g, 128, n, 4), np.uint8)
    nib[..., 0::2] = words & 0xF
    nib[..., 1::2] = words >> 4
    vals = E2M1[nib] * np.repeat(np.exp2(scales.astype(np.float64) - 127.0), 8, axis=1)[..., None]
    return vals.transpose(0, 1, 3, 2).reshape(g * 512, n)


K, T, N, U = 1024, 1024, 256, 2048


def setup_inputs():
    n = np.random.standard_normal
    s = mx_kscale(K)[:, None]
    packed_xT = pack_fp4(n((K, T)) * s)
    return {
        "x_words": packed_xT[0],
        "x_scales": packed_xT[1],
        "mem": n((N, U)).astype(np.float32),
        "w1": (n((K, N)) / np.sqrt(K) / s).astype(np.float32),
        "slot": striped(np.random.permutation(U)[:T]),
    }


def reference(x_words, x_scales, mem, w1, slot):
    xq = unpack_fp4(x_words, x_scales)
    y = mxq(f64(w1), 0, "e4m3").T @ xq
    out = f64(mem).copy()
    out[:, unstriped(slot)] = np.maximum(f64(mem)[:, unstriped(slot)], y)
    return out

@@ -1,0 +1,131 @@
+from contextlib import ExitStack
+
+import concourse.mybir as mybir
+
+K, T, N, U = 1024, 1024, 256, 2048
+FLOPS = 2 * K * T * N
+
+F32 = mybir.dt.float32
+BF16 = mybir.dt.bfloat16
+I32 = mybir.dt.int32
+U32 = mybir.dt.uint32
+U16 = mybir.dt.uint16
+U8 = mybir.dt.uint8
+FP8X4 = mybir.dt.float8_e4m3fn_x4
+FP4X4 = mybir.dt.float4_e2m1fn_x4
+MAX = mybir.AluOpType.max
+
+P = 128
+PACK = 4
+PASSES = K // (P * PACK)
+BLOCKS = N // P
+HALF = 512
+HALVES = T // HALF
+GROUP = 16
+
+
+def tile_picked_widxput_max_l_kernel(tc, x_words, x_scales, mem, w1, slot, out):
+    nc = tc.nc
+    with ExitStack() as ctx:
+        keep = ctx.enter_context(tc.tile_pool(name="keep", bufs=1))
+        psum = ctx.enter_context(tc.psum_pool(name="psum", bufs=1))
+
+        offsets = keep.tile([P, T // GROUP], U16, name="offsets")
+        window = [keep.tile([P, U], F32, name=f"window{b}") for b in range(BLOCKS)]
+        w_raw = [[keep.tile([P, PACK, P], F32, name=f"w_raw{b}{z}") for z in range(PASSES)] for b in range(BLOCKS)]
+        w_bf = [keep.tile([P, PASSES, P, PACK], BF16, name=f"w_bf{b}", align_bytes=64) for b in range(BLOCKS)]
+        w_codes = [keep.tile([P, PASSES, P], U32, name=f"w_codes{b}", align_bytes=64) for b in range(BLOCKS)]
+        w_scale = [keep.tile([P, PASSES, P], U8, name=f"w_scale{b}", align_bytes=64) for b in range(BLOCKS)]
+        x_codes = [keep.tile([P, PASSES, 2 * HALF], U8, name=f"x_codes{h}", align_bytes=64) for h in range(HALVES)]
+        x_scale = keep.tile([P, PASSES, T], U8, name="x_scale", align_bytes=64)
+        old = [keep.tile([P, T], F32, name=f"old{b}") for b in range(BLOCKS)]
+        new = [keep.tile([P, T], F32, name=f"new{b}") for b in range(BLOCKS)]
+        acc = [[psum.tile([P, HALF], F32, name=f"acc{b}{h}") for h in range(HALVES)] for b in range(BLOCKS)]
+
+        w_view = w1.rearrange("(z p j) m -> z p j m", p=P, j=PACK)
+        x_view = x_words.rearrange("z p c -> p z c")
+
+        def load_w(b):
+            for z in range(PASSES):
+                nc.sync.dma_start(w_raw[b][z][:], w_view[z, :, :, b * P:(b + 1) * P])
+
+        def load_x(h):
+            nc.sync.dma_start(x_codes[h][:].bitcast(I32), x_view[:, :, 2 * HALF * h:2 * HALF * (h + 1)].bitcast(I32))
+
+        def load_mem(b):
+            nc.sync.dma_start(window[b][:], mem[b * P:(b + 1) * P, :])
+
+        def cast(b, z, copy):
+            copy(w_bf[b][:, z].rearrange("p (c i) j -> p c j i", i=4), w_raw[b][z][:].rearrange("p j (c i) -> p c j i", i=4))
+
+        def quantise(b):
+            nc.vector.quantize_mx(
+                out=w_codes[b][:].rearrange("p z m -> p (z m)").bitcast(FP8X4),
+                scales=w_scale[b][:].rearrange("p z m -> p (z m)"),
+                in_=w_bf[b][:].rearrange("p z m j -> p (z m j)"),
+            )
+
+        def project(b, h):
+            for z in range(PASSES):
+                nc.tensor.matmul_mx(
+                    out=acc[b][h][:],
+                    lhsT=w_codes[b][:, z, :].bitcast(FP8X4),
+                    lhsT_scale=w_scale[b][:, z, :],
+                    rhs=x_codes[h][:, z, :].bitcast(FP4X4),
+                    rhs_scale=x_scale[:, z, h * HALF:(h + 1) * HALF],
+                    start=(z == 0),
+                    stop=(z == PASSES - 1),
+                )
+
+        def cols(lo, hi):
+            return offsets[:, lo // GROUP:hi // GROUP]
+
+        def gather(b, lo, hi):
+            nc.vector.tensor_copy(old[b][:, lo:hi], window[b][:].indirect(cols(lo, hi)))
+
+        def larger(b, h):
+            s = slice(h * HALF, (h + 1) * HALF)
+            nc.vector.tensor_tensor(new[b][:, s], acc[b][h][:], old[b][:, s], MAX)
+
+        def scatter(b, lo, hi):
+            nc.vector.tensor_copy(window[b][:].indirect(cols(lo, hi)), new[b][:, lo:hi])
+
+        def store(b):
+            nc.sync.dma_start(out[b * P:(b + 1) * P, :], window[b][:])
+
+        for q in range(4):
+            nc.scalar.dma_start(
+                x_scale[32 * q:32 * q + 4, :, :].bitcast(I32),
+                x_scales[:, 4 * q:4 * q + 4, :].rearrange("z r c -> r z c").bitcast(I32),
+            )
+        load_w(0)
+        nc.sync.dma_start(offsets[:], slot)
+        load_mem(0)
+        load_x(0)
+        load_x(1)
+        load_w(1)
+        load_mem(1)
+
+        for z in range(PASSES):
+            cast(0, z, nc.vector.tensor_copy)
+        quantise(0)
+        for h in range(HALVES):
+            project(0, h)
+        for z in range(PASSES):
+            cast(1, z, nc.scalar.copy)
+        gather(0, 0, HALF)
+        gather(0, HALF, T)
+        larger(0, 0)
+        larger(0, 1)
+        scatter(0, 0, HALF)
+        quantise(1)
+        for h in range(HALVES):
+            project(1, h)
+        gather(1, 0, HALF)
+        gather(1, HALF, T)
+        larger(1, 0)
+        larger(1, 1)
+        scatter(0, HALF, T)
+        store(0)
+        scatter(1, 0, T)
+        store(1)

@@ -36,21 +36,21 @@ def tile_picked_widxput_max_l_kernel(tc, x_words, x_scales, mem, w1, slot, out):
         w_bf = [keep.tile([P, PASSES, P, PACK], BF16, name=f"w_bf{b}", align_bytes=64) for b in range(BLOCKS)]
         w_codes = [keep.tile([P, PASSES, P], U32, name=f"w_codes{b}", align_bytes=64) for b in range(BLOCKS)]
         w_scale = [keep.tile([P, PASSES, P], U8, name=f"w_scale{b}", align_bytes=64) for b in range(BLOCKS)]
-        x_codes = [keep.tile([P, PASSES, 2 * HALF], U8, name=f"x_codes{h}", align_bytes=64) for h in range(HALVES)]
+        x_codes = [[keep.tile([P, 2 * HALF], U8, name=f"x_codes{h}{z}", align_bytes=64) for z in range(PASSES)] for h in range(HALVES)]
         x_scale = keep.tile([P, PASSES, T], U8, name="x_scale", align_bytes=64)
         old = [keep.tile([P, T], F32, name=f"old{b}") for b in range(BLOCKS)]
         new = [keep.tile([P, T], F32, name=f"new{b}") for b in range(BLOCKS)]
         acc = [[psum.tile([P, HALF], F32, name=f"acc{b}{h}") for h in range(HALVES)] for b in range(BLOCKS)]
 
         w_view = w1.rearrange("(z p j) m -> z p j m", p=P, j=PACK)
-        x_view = x_words.rearrange("z p c -> p z c")
 
         def load_w(b):
             for z in range(PASSES):
                 nc.sync.dma_start(w_raw[b][z][:], w_view[z, :, :, b * P:(b + 1) * P])
 
         def load_x(h):
-            nc.sync.dma_start(x_codes[h][:].bitcast(I32), x_view[:, :, 2 * HALF * h:2 * HALF * (h + 1)].bitcast(I32))
+            for z in range(PASSES):
+                nc.sync.dma_start(x_codes[h][z][:].bitcast(I32), x_words[z, :, 2 * HALF * h:2 * HALF * (h + 1)].bitcast(I32))
 
         def load_mem(b):
             nc.sync.dma_start(window[b][:], mem[b * P:(b + 1) * P, :])
@@ -71,7 +71,7 @@ def tile_picked_widxput_max_l_kernel(tc, x_words, x_scales, mem, w1, slot, out):
                     out=acc[b][h][:],
                     lhsT=w_codes[b][:, z, :].bitcast(FP8X4),
                     lhsT_scale=w_scale[b][:, z, :],
-                    rhs=x_codes[h][:, z, :].bitcast(FP4X4),
+                    rhs=x_codes[h][z][:].bitcast(FP4X4),
                     rhs_scale=x_scale[:, z, h * HALF:(h + 1) * HALF],
                     start=(z == 0),
                     stop=(z == PASSES - 1),
@@ -93,14 +93,14 @@ def tile_picked_widxput_max_l_kernel(tc, x_words, x_scales, mem, w1, slot, out):
         def store(b):
             nc.sync.dma_start(out[b * P:(b + 1) * P, :], window[b][:])
 
-        for q in range(4):
-            nc.scalar.dma_start(
-                x_scale[32 * q:32 * q + 4, :, :].bitcast(I32),
-                x_scales[:, 4 * q:4 * q + 4, :].rearrange("z r c -> r z c").bitcast(I32),
-            )
         load_w(0)
         nc.sync.dma_start(offsets[:], slot)
         load_mem(0)
+        for r in range(4):
+            nc.sync.dma_start(
+                x_scale[r:P:32, :, :].bitcast(I32),
+                x_scales.rearrange("z (q r) c -> r q z c", r=4)[r].bitcast(I32),
+            )
         load_x(0)
         load_x(1)
         load_w(1)

@@ -22,6 +22,7 @@ BLOCKS = N // P
 HALF = 512
 HALVES = T // HALF
 GROUP = 16
+FIRST = 640
 
 
 def tile_picked_widxput_max_l_kernel(tc, x_words, x_scales, mem, w1, slot, out):
@@ -32,50 +33,55 @@ def tile_picked_widxput_max_l_kernel(tc, x_words, x_scales, mem, w1, slot, out):
 
         offsets = keep.tile([P, T // GROUP], U16, name="offsets")
         window = [keep.tile([P, U], F32, name=f"window{b}") for b in range(BLOCKS)]
-        w_raw = [[keep.tile([P, PACK, P], F32, name=f"w_raw{b}{z}") for z in range(PASSES)] for b in range(BLOCKS)]
+        w_raw = [[keep.tile([P, PACK, P], F32, name=f"w_raw{b}{z}")[:] for z in range(PASSES)] for b in range(BLOCKS)]
         w_bf = [keep.tile([P, PASSES, P, PACK], BF16, name=f"w_bf{b}", align_bytes=64) for b in range(BLOCKS)]
         w_codes = [keep.tile([P, PASSES, P], U32, name=f"w_codes{b}", align_bytes=64) for b in range(BLOCKS)]
         w_scale = [keep.tile([P, PASSES, P], U8, name=f"w_scale{b}", align_bytes=64) for b in range(BLOCKS)]
         x_codes = [[keep.tile([P, 2 * HALF], U8, name=f"x_codes{h}{z}", align_bytes=64) for z in range(PASSES)] for h in range(HALVES)]
-        x_scale = keep.tile([P, PASSES, T], U8, name="x_scale", align_bytes=64)
-        old = [keep.tile([P, T], F32, name=f"old{b}") for b in range(BLOCKS)]
+        x_scale = [keep.tile([P, PASSES, HALF], U8, name=f"x_scale{h}", align_bytes=64) for h in range(HALVES)]
+        old = [keep.tile([P, FIRST + PACK * P], F32, name=f"old{b}") for b in range(BLOCKS)]
+        w_raw[0][1] = old[0][:, FIRST:].rearrange("p (j m) -> p j m", j=PACK)
         new = [keep.tile([P, T], F32, name=f"new{b}") for b in range(BLOCKS)]
         acc = [[psum.tile([P, HALF], F32, name=f"acc{b}{h}") for h in range(HALVES)] for b in range(BLOCKS)]
 
         w_view = w1.rearrange("(z p j) m -> z p j m", p=P, j=PACK)
 
-        def load_w(b):
-            for z in range(PASSES):
-                nc.sync.dma_start(w_raw[b][z][:], w_view[z, :, :, b * P:(b + 1) * P])
+        def load_w(b, z):
+            nc.sync.dma_start(w_raw[b][z], w_view[z, :, :, b * P:(b + 1) * P])
 
-        def load_x(h):
-            for z in range(PASSES):
-                nc.sync.dma_start(x_codes[h][z][:].bitcast(I32), x_words[z, :, 2 * HALF * h:2 * HALF * (h + 1)].bitcast(I32))
+        def load_scales(h):
+            for r in range(4):
+                nc.sync.dma_start(
+                    x_scale[h][r:P:32, :, :].bitcast(I32),
+                    x_scales.rearrange("z (q r) c -> r q z c", r=4)[r][:, :, h * HALF:(h + 1) * HALF].bitcast(I32),
+                )
+
+        def load_x(h, z):
+            nc.sync.dma_start(x_codes[h][z][:].bitcast(I32), x_words[z, :, 2 * HALF * h:2 * HALF * (h + 1)].bitcast(I32))
 
         def load_mem(b):
             nc.sync.dma_start(window[b][:], mem[b * P:(b + 1) * P, :])
 
         def cast(b, z, copy):
-            copy(w_bf[b][:, z].rearrange("p (c i) j -> p c j i", i=4), w_raw[b][z][:].rearrange("p j (c i) -> p c j i", i=4))
+            copy(w_bf[b][:, z].rearrange("p (c i) j -> p c j i", i=4), w_raw[b][z].rearrange("p j (c i) -> p c j i", i=4))
 
-        def quantise(b):
+        def quantise(b, z0, z1):
             nc.vector.quantize_mx(
-                out=w_codes[b][:].rearrange("p z m -> p (z m)").bitcast(FP8X4),
-                scales=w_scale[b][:].rearrange("p z m -> p (z m)"),
-                in_=w_bf[b][:].rearrange("p z m j -> p (z m j)"),
+                out=w_codes[b][:, z0:z1].rearrange("p z m -> p (z m)").bitcast(FP8X4),
+                scales=w_scale[b][:, z0:z1].rearrange("p z m -> p (z m)"),
+                in_=w_bf[b][:, z0:z1].rearrange("p z m j -> p (z m j)"),
             )
 
-        def project(b, h):
-            for z in range(PASSES):
-                nc.tensor.matmul_mx(
-                    out=acc[b][h][:],
-                    lhsT=w_codes[b][:, z, :].bitcast(FP8X4),
-                    lhsT_scale=w_scale[b][:, z, :],
-                    rhs=x_codes[h][z][:].bitcast(FP4X4),
-                    rhs_scale=x_scale[:, z, h * HALF:(h + 1) * HALF],
-                    start=(z == 0),
-                    stop=(z == PASSES - 1),
-                )
+        def project(b, h, z):
+            nc.tensor.matmul_mx(
+                out=acc[b][h][:],
+                lhsT=w_codes[b][:, z, :].bitcast(FP8X4),
+                lhsT_scale=w_scale[b][:, z, :],
+                rhs=x_codes[h][z][:].bitcast(FP4X4),
+                rhs_scale=x_scale[h][:, z, :],
+                start=(z == 0),
+                stop=(z == PASSES - 1),
+            )
 
         def cols(lo, hi):
             return offsets[:, lo // GROUP:hi // GROUP]
@@ -93,37 +99,43 @@ def tile_picked_widxput_max_l_kernel(tc, x_words, x_scales, mem, w1, slot, out):
         def store(b):
             nc.sync.dma_start(out[b * P:(b + 1) * P, :], window[b][:])
 
-        load_w(0)
+        load_w(0, 0)
         nc.sync.dma_start(offsets[:], slot)
         load_mem(0)
-        for r in range(4):
-            nc.sync.dma_start(
-                x_scale[r:P:32, :, :].bitcast(I32),
-                x_scales.rearrange("z (q r) c -> r q z c", r=4)[r].bitcast(I32),
-            )
-        load_x(0)
-        load_x(1)
-        load_w(1)
+        load_w(0, 1)
+        load_scales(0)
+        load_x(0, 0)
+        load_x(0, 1)
+        load_scales(1)
+        load_x(1, 0)
+        load_w(1, 0)
+        load_w(1, 1)
         load_mem(1)
+        load_x(1, 1)
 
+        cast(0, 0, nc.vector.tensor_copy)
+        quantise(0, 0, 1)
+        cast(0, 1, nc.scalar.copy)
+        gather(0, 0, FIRST)
+        quantise(0, 1, 2)
+        gather(0, FIRST, T)
         for z in range(PASSES):
-            cast(0, z, nc.vector.tensor_copy)
-        quantise(0)
-        for h in range(HALVES):
-            project(0, h)
+            project(0, 0, z)
         for z in range(PASSES):
             cast(1, z, nc.scalar.copy)
-        gather(0, 0, HALF)
-        gather(0, HALF, T)
+        project(0, 1, 0)
         larger(0, 0)
-        larger(0, 1)
         scatter(0, 0, HALF)
-        quantise(1)
-        for h in range(HALVES):
-            project(1, h)
+        quantise(1, 0, 2)
+        for z in range(PASSES):
+            project(1, 0, z)
         gather(1, 0, HALF)
         gather(1, HALF, T)
         larger(1, 0)
+        project(1, 1, 0)
+        project(0, 1, 1)
+        project(1, 1, 1)
+        larger(0, 1)
         larger(1, 1)
         scatter(0, HALF, T)
         store(0)

@@ -49,9 +49,9 @@ def tile_picked_widxput_max_l_kernel(tc, x_words, x_scales, mem, w1, slot, out):
         def load_w(b, z):
             nc.sync.dma_start(w_raw[b][z], w_view[z, :, :, b * P:(b + 1) * P])
 
-        def load_scales(h):
+        def load_scales(h, queue):
             for r in range(4):
-                nc.sync.dma_start(
+                queue.dma_start(
                     x_scale[h][r:P:32, :, :].bitcast(I32),
                     x_scales.rearrange("z (q r) c -> r q z c", r=4)[r][:, :, h * HALF:(h + 1) * HALF].bitcast(I32),
                 )
@@ -99,14 +99,14 @@ def tile_picked_widxput_max_l_kernel(tc, x_words, x_scales, mem, w1, slot, out):
         def store(b):
             nc.sync.dma_start(out[b * P:(b + 1) * P, :], window[b][:])
 
+        load_scales(0, nc.scalar)
         load_w(0, 0)
         nc.sync.dma_start(offsets[:], slot)
         load_mem(0)
         load_w(0, 1)
-        load_scales(0)
         load_x(0, 0)
         load_x(0, 1)
-        load_scales(1)
+        load_scales(1, nc.sync)
         load_x(1, 0)
         load_w(1, 0)
         load_w(1, 1)

@@ -106,9 +106,9 @@ def tile_picked_widxput_max_l_kernel(tc, x_words, x_scales, mem, w1, slot, out):
         load_w(0, 1)
         load_x(0, 0)
         load_x(0, 1)
+        load_w(1, 0)
         load_scales(1, nc.sync)
         load_x(1, 0)
-        load_w(1, 0)
         load_w(1, 1)
         load_mem(1)
         load_x(1, 1)
@@ -125,8 +125,9 @@ def tile_picked_widxput_max_l_kernel(tc, x_words, x_scales, mem, w1, slot, out):
             cast(1, z, nc.scalar.copy)
         project(0, 1, 0)
         larger(0, 0)
+        quantise(1, 0, 1)
         scatter(0, 0, HALF)
-        quantise(1, 0, 2)
+        quantise(1, 1, 2)
         for z in range(PASSES):
             project(1, 0, z)
         gather(1, 0, HALF)

@@ -22,7 +22,7 @@ BLOCKS = N // P
 HALF = 512
 HALVES = T // HALF
 GROUP = 16
-FIRST = 640
+FIRST = 768
 
 
 def tile_picked_widxput_max_l_kernel(tc, x_words, x_scales, mem, w1, slot, out):
@@ -43,6 +43,7 @@ def tile_picked_widxput_max_l_kernel(tc, x_words, x_scales, mem, w1, slot, out):
         w_raw[0][1] = old[0][:, FIRST:].rearrange("p (j m) -> p j m", j=PACK)
         new = [keep.tile([P, T], F32, name=f"new{b}") for b in range(BLOCKS)]
         acc = [[psum.tile([P, HALF], F32, name=f"acc{b}{h}") for h in range(HALVES)] for b in range(BLOCKS)]
+        lead = [acc[0][0]] + [psum.tile([P, HALF], F32, name=f"lead{g}") for g in range(1, HALF // P)]
 
         w_view = w1.rearrange("(z p j) m -> z p j m", p=P, j=PACK)
 
@@ -79,6 +80,17 @@ def tile_picked_widxput_max_l_kernel(tc, x_words, x_scales, mem, w1, slot, out):
                 lhsT_scale=w_scale[b][:, z, :],
                 rhs=x_codes[h][z][:].bitcast(FP4X4),
                 rhs_scale=x_scale[h][:, z, :],
+                start=(z == 0),
+                stop=(z == PASSES - 1),
+            )
+
+        def project_lead(g, z):
+            nc.tensor.matmul_mx(
+                out=lead[g][:, :P],
+                lhsT=w_codes[0][:, z, :].bitcast(FP8X4),
+                lhsT_scale=w_scale[0][:, z, :],
+                rhs=x_codes[0][z][:, 2 * P * g:2 * P * (g + 1)].bitcast(FP4X4),
+                rhs_scale=x_scale[0][:, z, P * g:P * (g + 1)],
                 start=(z == 0),
                 stop=(z == PASSES - 1),
             )
@@ -120,11 +132,14 @@ def tile_picked_widxput_max_l_kernel(tc, x_words, x_scales, mem, w1, slot, out):
         quantise(0, 1, 2)
         gather(0, FIRST, T)
         for z in range(PASSES):
-            project(0, 0, z)
+            for g in range(HALF // P):
+                project_lead(g, z)
         for z in range(PASSES):
             cast(1, z, nc.scalar.copy)
         project(0, 1, 0)
-        larger(0, 0)
+        for g in range(HALF // P):
+            s = slice(g * P, (g + 1) * P)
+            nc.vector.tensor_tensor(new[0][:, s], lead[g][:, :P], old[0][:, s], MAX)
         quantise(1, 0, 1)
         scatter(0, 0, HALF)
         quantise(1, 1, 2)

@@ -22,7 +22,7 @@ BLOCKS = N // P
 HALF = 512
 HALVES = T // HALF
 GROUP = 16
-FIRST = 768
+FIRST = 640
 
 
 def tile_picked_widxput_max_l_kernel(tc, x_words, x_scales, mem, w1, slot, out):
@@ -33,14 +33,16 @@ def tile_picked_widxput_max_l_kernel(tc, x_words, x_scales, mem, w1, slot, out):
 
         offsets = keep.tile([P, T // GROUP], U16, name="offsets")
         window = [keep.tile([P, U], F32, name=f"window{b}") for b in range(BLOCKS)]
-        w_raw = [[keep.tile([P, PACK, P], F32, name=f"w_raw{b}{z}")[:] for z in range(PASSES)] for b in range(BLOCKS)]
         w_bf = [keep.tile([P, PASSES, P, PACK], BF16, name=f"w_bf{b}", align_bytes=64) for b in range(BLOCKS)]
         w_codes = [keep.tile([P, PASSES, P], U32, name=f"w_codes{b}", align_bytes=64) for b in range(BLOCKS)]
         w_scale = [keep.tile([P, PASSES, P], U8, name=f"w_scale{b}", align_bytes=64) for b in range(BLOCKS)]
         x_codes = [[keep.tile([P, 2 * HALF], U8, name=f"x_codes{h}{z}", align_bytes=64) for z in range(PASSES)] for h in range(HALVES)]
         x_scale = [keep.tile([P, PASSES, HALF], U8, name=f"x_scale{h}", align_bytes=64) for h in range(HALVES)]
-        old = [keep.tile([P, FIRST + PACK * P], F32, name=f"old{b}") for b in range(BLOCKS)]
-        w_raw[0][1] = old[0][:, FIRST:].rearrange("p (j m) -> p j m", j=PACK)
+        old = [keep.tile([P, FIRST + PACK * P], F32, name="old0"), keep.tile([P, T], F32, name="old1")]
+        w_raw = [
+            [keep.tile([P, PACK, P], F32, name="w_raw00")[:], old[0][:, FIRST:].rearrange("p (j m) -> p j m", j=PACK)],
+            [keep.tile([P, PACK, P], F32, name=f"w_raw1{z}")[:] for z in range(PASSES)],
+        ]
         new = [keep.tile([P, T], F32, name=f"new{b}") for b in range(BLOCKS)]
         acc = [[psum.tile([P, HALF], F32, name=f"acc{b}{h}") for h in range(HALVES)] for b in range(BLOCKS)]
         lead = [acc[0][0]] + [psum.tile([P, HALF], F32, name=f"lead{g}") for g in range(1, HALF // P)]

@@ -18,11 +18,16 @@ MAX = mybir.AluOpType.max
 P = 128
 PACK = 4
 PASSES = K // (P * PACK)
-BLOCKS = N // P
+ROW_GROUPS = N // P
 HALF = 512
 HALVES = T // HALF
-GROUP = 16
+NARROW = HALF // P
+STRIPE = 16
+QUADRANT = 32
+SCALE_ROWS = 4
+RUN = 4
 FIRST = 640
+EARLY = HALF - P
 
 
 def tile_picked_widxput_max_l_kernel(tc, x_words, x_scales, mem, w1, slot, out):
@@ -31,32 +36,32 @@ def tile_picked_widxput_max_l_kernel(tc, x_words, x_scales, mem, w1, slot, out):
         keep = ctx.enter_context(tc.tile_pool(name="keep", bufs=1))
         psum = ctx.enter_context(tc.psum_pool(name="psum", bufs=1))
 
-        offsets = keep.tile([P, T // GROUP], U16, name="offsets")
-        window = [keep.tile([P, U], F32, name=f"window{b}") for b in range(BLOCKS)]
-        w_bf = [keep.tile([P, PASSES, P, PACK], BF16, name=f"w_bf{b}", align_bytes=64) for b in range(BLOCKS)]
-        w_codes = [keep.tile([P, PASSES, P], U32, name=f"w_codes{b}", align_bytes=64) for b in range(BLOCKS)]
-        w_scale = [keep.tile([P, PASSES, P], U8, name=f"w_scale{b}", align_bytes=64) for b in range(BLOCKS)]
+        offsets = keep.tile([P, T // STRIPE], U16, name="offsets")
+        window = [keep.tile([P, U], F32, name=f"window{b}") for b in range(ROW_GROUPS)]
+        w_bf = [keep.tile([P, PASSES, P, PACK], BF16, name=f"w_bf{b}", align_bytes=64) for b in range(ROW_GROUPS)]
+        w_codes = [keep.tile([P, PASSES, P], U32, name=f"w_codes{b}", align_bytes=64) for b in range(ROW_GROUPS)]
+        w_scale = [keep.tile([P, PASSES, P], U8, name=f"w_scale{b}", align_bytes=64) for b in range(ROW_GROUPS)]
         x_codes = [[keep.tile([P, 2 * HALF], U8, name=f"x_codes{h}{z}", align_bytes=64) for z in range(PASSES)] for h in range(HALVES)]
         x_scale = [keep.tile([P, PASSES, HALF], U8, name=f"x_scale{h}", align_bytes=64) for h in range(HALVES)]
         old = [keep.tile([P, FIRST + PACK * P], F32, name="old0"), keep.tile([P, T], F32, name="old1")]
         w_raw = [
-            [keep.tile([P, PACK, P], F32, name="w_raw00")[:], old[0][:, FIRST:].rearrange("p (j m) -> p j m", j=PACK)],
+            [keep.tile([P, PACK, P], F32, name="w_raw00")[:], old[0][:, FIRST:].rearrange("p (t m) -> p t m", t=PACK)],
             [keep.tile([P, PACK, P], F32, name=f"w_raw1{z}")[:] for z in range(PASSES)],
         ]
-        new = [keep.tile([P, T], F32, name=f"new{b}") for b in range(BLOCKS)]
-        acc = [[psum.tile([P, HALF], F32, name=f"acc{b}{h}") for h in range(HALVES)] for b in range(BLOCKS)]
-        lead = [acc[0][0]] + [psum.tile([P, HALF], F32, name=f"lead{g}") for g in range(1, HALF // P)]
+        new = [keep.tile([P, T], F32, name=f"new{b}") for b in range(ROW_GROUPS)]
+        acc = [[psum.tile([P, HALF], F32, name=f"acc{b}{h}") for h in range(HALVES)] for b in range(ROW_GROUPS)]
+        narrow_acc = [acc[0][0]] + [psum.tile([P, HALF], F32, name=f"narrow_acc{g}") for g in range(1, NARROW)]
 
-        w_view = w1.rearrange("(z p j) m -> z p j m", p=P, j=PACK)
+        w_view = w1.rearrange("(z p t) m -> z p t m", p=P, t=PACK)
 
         def load_w(b, z):
             nc.sync.dma_start(w_raw[b][z], w_view[z, :, :, b * P:(b + 1) * P])
 
         def load_scales(h, queue):
-            for r in range(4):
+            for r in range(SCALE_ROWS):
                 queue.dma_start(
-                    x_scale[h][r:P:32, :, :].bitcast(I32),
-                    x_scales.rearrange("z (q r) c -> r q z c", r=4)[r][:, :, h * HALF:(h + 1) * HALF].bitcast(I32),
+                    x_scale[h][r:P:QUADRANT, :, :].bitcast(I32),
+                    x_scales.rearrange("z (q r) c -> r q z c", r=SCALE_ROWS)[r][:, :, h * HALF:(h + 1) * HALF].bitcast(I32),
                 )
 
         def load_x(h, z):
@@ -65,50 +70,38 @@ def tile_picked_widxput_max_l_kernel(tc, x_words, x_scales, mem, w1, slot, out):
         def load_mem(b):
             nc.sync.dma_start(window[b][:], mem[b * P:(b + 1) * P, :])
 
-        def cast(b, z, copy):
-            copy(w_bf[b][:, z].rearrange("p (c i) j -> p c j i", i=4), w_raw[b][z].rearrange("p j (c i) -> p c j i", i=4))
+        def round_w(b, z, copy):
+            copy(w_bf[b][:, z].rearrange("p (c i) t -> p c t i", i=RUN), w_raw[b][z].rearrange("p t (c i) -> p c t i", i=RUN))
 
-        def quantise(b, z0, z1):
+        def quantise(b, z):
             nc.vector.quantize_mx(
-                out=w_codes[b][:, z0:z1].rearrange("p z m -> p (z m)").bitcast(FP8X4),
-                scales=w_scale[b][:, z0:z1].rearrange("p z m -> p (z m)"),
-                in_=w_bf[b][:, z0:z1].rearrange("p z m j -> p (z m j)"),
+                out=w_codes[b][:, z:z + 1].rearrange("p z m -> p (z m)").bitcast(FP8X4),
+                scales=w_scale[b][:, z:z + 1].rearrange("p z m -> p (z m)"),
+                in_=w_bf[b][:, z:z + 1].rearrange("p z m t -> p (z m t)"),
             )
 
-        def project(b, h, z):
+        def project(bank, b, h, z, lo, hi):
             nc.tensor.matmul_mx(
-                out=acc[b][h][:],
+                out=bank[:, :hi - lo],
                 lhsT=w_codes[b][:, z, :].bitcast(FP8X4),
                 lhsT_scale=w_scale[b][:, z, :],
-                rhs=x_codes[h][z][:].bitcast(FP4X4),
-                rhs_scale=x_scale[h][:, z, :],
+                rhs=x_codes[h][z][:, 2 * lo:2 * hi].bitcast(FP4X4),
+                rhs_scale=x_scale[h][:, z, lo:hi],
                 start=(z == 0),
                 stop=(z == PASSES - 1),
             )
 
-        def project_lead(g, z):
-            nc.tensor.matmul_mx(
-                out=lead[g][:, :P],
-                lhsT=w_codes[0][:, z, :].bitcast(FP8X4),
-                lhsT_scale=w_scale[0][:, z, :],
-                rhs=x_codes[0][z][:, 2 * P * g:2 * P * (g + 1)].bitcast(FP4X4),
-                rhs_scale=x_scale[0][:, z, P * g:P * (g + 1)],
-                start=(z == 0),
-                stop=(z == PASSES - 1),
-            )
-
-        def cols(lo, hi):
-            return offsets[:, lo // GROUP:hi // GROUP]
+        def listed(b, lo, hi):
+            return window[b][:].indirect(offsets[:, lo // STRIPE:hi // STRIPE])
 
         def gather(b, lo, hi):
-            nc.vector.tensor_copy(old[b][:, lo:hi], window[b][:].indirect(cols(lo, hi)))
+            nc.vector.tensor_copy(old[b][:, lo:hi], listed(b, lo, hi))
 
-        def larger(b, h):
-            s = slice(h * HALF, (h + 1) * HALF)
-            nc.vector.tensor_tensor(new[b][:, s], acc[b][h][:], old[b][:, s], MAX)
+        def larger(bank, b, lo, hi):
+            nc.vector.tensor_tensor(new[b][:, lo:hi], bank[:, :hi - lo], old[b][:, lo:hi], MAX)
 
         def scatter(b, lo, hi):
-            nc.vector.tensor_copy(window[b][:].indirect(cols(lo, hi)), new[b][:, lo:hi])
+            nc.vector.tensor_copy(listed(b, lo, hi), new[b][:, lo:hi])
 
         def store(b):
             nc.sync.dma_start(out[b * P:(b + 1) * P, :], window[b][:])
@@ -118,44 +111,44 @@ def tile_picked_widxput_max_l_kernel(tc, x_words, x_scales, mem, w1, slot, out):
         nc.sync.dma_start(offsets[:], slot)
         load_mem(0)
         load_w(0, 1)
-        load_x(0, 0)
-        load_x(0, 1)
+        for z in range(PASSES):
+            load_x(0, z)
         load_w(1, 0)
         load_scales(1, nc.sync)
-        load_x(1, 0)
         load_w(1, 1)
         load_mem(1)
+        load_x(1, 0)
         load_x(1, 1)
 
-        cast(0, 0, nc.vector.tensor_copy)
-        quantise(0, 0, 1)
-        cast(0, 1, nc.scalar.copy)
+        round_w(0, 0, nc.vector.tensor_copy)
+        quantise(0, 0)
+        round_w(0, 1, nc.scalar.copy)
         gather(0, 0, FIRST)
-        quantise(0, 1, 2)
+        quantise(0, 1)
         gather(0, FIRST, T)
         for z in range(PASSES):
-            for g in range(HALF // P):
-                project_lead(g, z)
+            for g in range(NARROW):
+                project(narrow_acc[g], 0, 0, z, g * P, (g + 1) * P)
         for z in range(PASSES):
-            cast(1, z, nc.scalar.copy)
-        project(0, 1, 0)
-        for g in range(HALF // P):
-            s = slice(g * P, (g + 1) * P)
-            nc.vector.tensor_tensor(new[0][:, s], lead[g][:, :P], old[0][:, s], MAX)
-        quantise(1, 0, 1)
-        scatter(0, 0, HALF)
-        quantise(1, 1, 2)
+            round_w(1, z, nc.scalar.copy)
+        project(acc[0][1], 0, 1, 0, 0, HALF)
+        for g in range(NARROW):
+            larger(narrow_acc[g], 0, g * P, (g + 1) * P)
+        quantise(1, 0)
+        scatter(0, 0, EARLY)
+        quantise(1, 1)
+
         for z in range(PASSES):
-            project(1, 0, z)
+            project(acc[1][0], 1, 0, z, 0, HALF)
         gather(1, 0, HALF)
         gather(1, HALF, T)
-        larger(1, 0)
-        project(1, 1, 0)
-        project(0, 1, 1)
-        project(1, 1, 1)
-        larger(0, 1)
-        larger(1, 1)
-        scatter(0, HALF, T)
+        larger(acc[1][0], 1, 0, HALF)
+        project(acc[1][1], 1, 1, 0, 0, HALF)
+        for b in range(ROW_GROUPS):
+            project(acc[b][1], b, 1, 1, 0, HALF)
+        for b in range(ROW_GROUPS):
+            larger(acc[b][1], b, HALF, T)
+        scatter(0, EARLY, T)
         store(0)
         scatter(1, 0, T)
         store(1)

@@ -122,7 +122,11 @@ def tile_picked_widxput_max_l_kernel(tc, x_words, x_scales, mem, w1, slot, out):
 
         round_w(0, 0, nc.vector.tensor_copy)
         quantise(0, 0)
-        round_w(0, 1, nc.scalar.copy)
+        rounded = w_bf[0][:, 1].rearrange("p (c i) t -> p c t i", i=RUN)
+        staged = w_raw[0][1].rearrange("p t (c i) -> p c t i", i=RUN)
+        share = 3 * P // (4 * RUN)
+        nc.scalar.copy(rounded[:, :share], staged[:, :share])
+        nc.gpsimd.tensor_scalar(rounded[:, share:], staged[:, share:], 1.0, 0.0, mybir.AluOpType.mult, mybir.AluOpType.add)
         gather(0, 0, FIRST)
         quantise(0, 1)
         gather(0, FIRST, T)

@@ -14,6 +14,9 @@ U8 = mybir.dt.uint8
 FP8X4 = mybir.dt.float8_e4m3fn_x4
 FP4X4 = mybir.dt.float4_e2m1fn_x4
 MAX = mybir.AluOpType.max
+ALU = mybir.AluOpType
+ACT = mybir.ActivationFunctionType
+LOWEST = -3.4028234663852886e38
 
 P = 128
 PACK = 4
@@ -28,6 +31,7 @@ SCALE_ROWS = 4
 RUN = 4
 FIRST = 640
 EARLY = HALF - P
+MASKED = 640
 
 
 def tile_picked_widxput_max_l_kernel(tc, x_words, x_scales, mem, w1, slot, out):
@@ -38,12 +42,12 @@ def tile_picked_widxput_max_l_kernel(tc, x_words, x_scales, mem, w1, slot, out):
 
         offsets = keep.tile([P, T // STRIPE], U16, name="offsets")
         window = [keep.tile([P, U], F32, name=f"window{b}") for b in range(ROW_GROUPS)]
-        w_bf = [keep.tile([P, PASSES, P, PACK], BF16, name=f"w_bf{b}", align_bytes=64) for b in range(ROW_GROUPS)]
+        w_bf = [[keep.tile([P, P, PACK], BF16, name=f"w_bf{b}{z}", tag=f"w_bf{b}{z}", align_bytes=64) for z in range(PASSES)] for b in range(ROW_GROUPS)]
         w_codes = [keep.tile([P, PASSES, P], U32, name=f"w_codes{b}", align_bytes=64) for b in range(ROW_GROUPS)]
         w_scale = [keep.tile([P, PASSES, P], U8, name=f"w_scale{b}", align_bytes=64) for b in range(ROW_GROUPS)]
         x_codes = [[keep.tile([P, 2 * HALF], U8, name=f"x_codes{h}{z}", align_bytes=64) for z in range(PASSES)] for h in range(HALVES)]
         x_scale = [keep.tile([P, PASSES, HALF], U8, name=f"x_scale{h}", align_bytes=64) for h in range(HALVES)]
-        old = [keep.tile([P, FIRST + PACK * P], F32, name="old0"), keep.tile([P, T], F32, name="old1")]
+        old = [keep.tile([P, FIRST + PACK * P], F32, name="old0"), keep.tile([P, P + T], F32, name="old1")]
         w_raw = [
             [keep.tile([P, PACK, P], F32, name="w_raw00")[:], old[0][:, FIRST:].rearrange("p (t m) -> p t m", t=PACK)],
             [keep.tile([P, PACK, P], F32, name=f"w_raw1{z}")[:] for z in range(PASSES)],
@@ -51,6 +55,9 @@ def tile_picked_widxput_max_l_kernel(tc, x_words, x_scales, mem, w1, slot, out):
         new = [keep.tile([P, T], F32, name=f"new{b}") for b in range(ROW_GROUPS)]
         acc = [[psum.tile([P, HALF], F32, name=f"acc{b}{h}") for h in range(HALVES)] for b in range(ROW_GROUPS)]
         narrow_acc = [acc[0][0]] + [psum.tile([P, HALF], F32, name=f"narrow_acc{g}") for g in range(1, NARROW)]
+
+        def spare(name, tag=None):
+            return keep.tile([P, HALF], F32, name=name, tag=tag or name, align_bytes=64)
 
         w_view = w1.rearrange("(z p t) m -> z p t m", p=P, t=PACK)
 
@@ -64,20 +71,20 @@ def tile_picked_widxput_max_l_kernel(tc, x_words, x_scales, mem, w1, slot, out):
                     x_scales.rearrange("z (q r) c -> r q z c", r=SCALE_ROWS)[r][:, :, h * HALF:(h + 1) * HALF].bitcast(I32),
                 )
 
-        def load_x(h, z):
-            nc.sync.dma_start(x_codes[h][z][:].bitcast(I32), x_words[z, :, 2 * HALF * h:2 * HALF * (h + 1)].bitcast(I32))
+        def load_x(h, z, lo=0, hi=HALF):
+            nc.sync.dma_start(x_codes[h][z][:, 2 * lo:2 * hi].bitcast(I32), x_words[z, :, 2 * (HALF * h + lo):2 * (HALF * h + hi)].bitcast(I32))
 
         def load_mem(b):
             nc.sync.dma_start(window[b][:], mem[b * P:(b + 1) * P, :])
 
         def round_w(b, z, copy):
-            copy(w_bf[b][:, z].rearrange("p (c i) t -> p c t i", i=RUN), w_raw[b][z].rearrange("p t (c i) -> p c t i", i=RUN))
+            copy(w_bf[b][z][:].rearrange("p (c i) t -> p c t i", i=RUN), w_raw[b][z].rearrange("p t (c i) -> p c t i", i=RUN))
 
         def quantise(b, z):
             nc.vector.quantize_mx(
                 out=w_codes[b][:, z:z + 1].rearrange("p z m -> p (z m)").bitcast(FP8X4),
                 scales=w_scale[b][:, z:z + 1].rearrange("p z m -> p (z m)"),
-                in_=w_bf[b][:, z:z + 1].rearrange("p z m t -> p (z m t)"),
+                in_=w_bf[b][z][:].rearrange("p m t -> p (m t)"),
             )
 
         def project(bank, b, h, z, lo, hi):
@@ -115,14 +122,15 @@ def tile_picked_widxput_max_l_kernel(tc, x_words, x_scales, mem, w1, slot, out):
             load_x(0, z)
         load_w(1, 0)
         load_scales(1, nc.sync)
+        load_x(1, 0)
+        load_x(1, 1, 0, HALF // 2)
         load_w(1, 1)
         load_mem(1)
-        load_x(1, 0)
-        load_x(1, 1)
+        load_x(1, 1, HALF // 2, HALF)
 
         round_w(0, 0, nc.vector.tensor_copy)
         quantise(0, 0)
-        rounded = w_bf[0][:, 1].rearrange("p (c i) t -> p c t i", i=RUN)
+        rounded = w_bf[0][1][:].rearrange("p (c i) t -> p c t i", i=RUN)
         staged = w_raw[0][1].rearrange("p t (c i) -> p c t i", i=RUN)
         share = 3 * P // (4 * RUN)
         nc.scalar.copy(rounded[:, :share], staged[:, :share])
@@ -141,18 +149,34 @@ def tile_picked_widxput_max_l_kernel(tc, x_words, x_scales, mem, w1, slot, out):
         quantise(1, 0)
         scatter(0, 0, EARLY)
         quantise(1, 1)
-
         for z in range(PASSES):
             project(acc[1][0], 1, 0, z, 0, HALF)
-        gather(1, 0, HALF)
-        gather(1, HALF, T)
-        larger(acc[1][0], 1, 0, HALF)
-        project(acc[1][1], 1, 1, 0, 0, HALF)
-        for b in range(ROW_GROUPS):
-            project(acc[b][1], b, 1, 1, 0, HALF)
-        for b in range(ROW_GROUPS):
-            larger(acc[b][1], b, HALF, T)
+            project(narrow_acc[0], 1, 1, z, 0, P)
+        for g in reversed(range(1, NARROW)):
+            for z in range(PASSES):
+                project(acc[1][1][:, (g - 1) * P:], 1, 1, z, g * P, (g + 1) * P)
+        project(acc[0][1], 0, 1, 1, 0, HALF)
+
+        gather(1, MASKED, T)
+        gather(1, 0, MASKED)
+        larger(acc[1][1], 1, MASKED, T)
+        larger(acc[0][1], 0, HALF, T)
+        scatter(1, MASKED, T)
         scatter(0, EARLY, T)
         store(0)
-        scatter(1, 0, T)
+
+        both, mask, part = [keep.tile([P, 2, MASKED], F32, name=name) for name in ("both", "mask", "part")]
+        gap, sign = [keep.tile([P, MASKED], F32, name=name) for name in ("gap", "sign")]
+        pieces = [slice(0, 2 * P), slice(2 * P, MASKED)]
+        nc.scalar.copy(both[:, 1, :HALF], acc[1][0][:])
+        nc.scalar.copy(both[:, 1, HALF:], narrow_acc[0][:, :P])
+        for c in pieces:
+            nc.gpsimd.tensor_tensor(gap[:, c], old[1][:, c], both[:, 1, c], ALU.subtract)
+        nc.gpsimd.tensor_scalar(both[:, 0, :], old[1][:, :MASKED], float("inf"), LOWEST, ALU.min, ALU.max)
+        for c in pieces:
+            nc.scalar.activation(sign[:, c], gap[:, c], ACT.Sign)
+            nc.scalar.activation(mask[:, 0, c], sign[:, c], ACT.Copy, bias=0.5, scale=0.5)
+            nc.scalar.activation(mask[:, 1, c], sign[:, c], ACT.Copy, bias=0.5, scale=-0.5)
+            nc.gpsimd.tensor_tensor(part[:, :, c], both[:, :, c], mask[:, :, c], ALU.mult)
+        nc.vector.tensor_tensor(listed(1, 0, MASKED), part[:, 0, :], part[:, 1, :], ALU.add)
         store(1)

@@ -14,9 +14,7 @@ U8 = mybir.dt.uint8
 FP8X4 = mybir.dt.float8_e4m3fn_x4
 FP4X4 = mybir.dt.float4_e2m1fn_x4
 MAX = mybir.AluOpType.max
-ALU = mybir.AluOpType
-ACT = mybir.ActivationFunctionType
-LOWEST = -3.4028234663852886e38
+COPY = mybir.ActivationFunctionType.Copy
 
 P = 128
 PACK = 4
@@ -24,14 +22,16 @@ PASSES = K // (P * PACK)
 ROW_GROUPS = N // P
 HALF = 512
 HALVES = T // HALF
-NARROW = HALF // P
 STRIPE = 16
 QUADRANT = 32
 SCALE_ROWS = 4
 RUN = 4
-FIRST = 640
-EARLY = HALF - P
-MASKED = 640
+FIRST = 256
+PIECE = 384
+VECTOR_FIRST = 480
+ROUND_SPLIT = 192
+SPLIT = 672
+MERGE = [512, 512, 512, 512]
 
 
 def tile_picked_widxput_max_l_kernel(tc, x_words, x_scales, mem, w1, slot, out):
@@ -42,141 +42,110 @@ def tile_picked_widxput_max_l_kernel(tc, x_words, x_scales, mem, w1, slot, out):
 
         offsets = keep.tile([P, T // STRIPE], U16, name="offsets")
         window = [keep.tile([P, U], F32, name=f"window{b}") for b in range(ROW_GROUPS)]
-        w_bf = [[keep.tile([P, P, PACK], BF16, name=f"w_bf{b}{z}", tag=f"w_bf{b}{z}", align_bytes=64) for z in range(PASSES)] for b in range(ROW_GROUPS)]
-        w_codes = [keep.tile([P, PASSES, P], U32, name=f"w_codes{b}", align_bytes=64) for b in range(ROW_GROUPS)]
-        w_scale = [keep.tile([P, PASSES, P], U8, name=f"w_scale{b}", align_bytes=64) for b in range(ROW_GROUPS)]
-        x_codes = [[keep.tile([P, 2 * HALF], U8, name=f"x_codes{h}{z}", align_bytes=64) for z in range(PASSES)] for h in range(HALVES)]
-        x_scale = [keep.tile([P, PASSES, HALF], U8, name=f"x_scale{h}", align_bytes=64) for h in range(HALVES)]
-        old = [keep.tile([P, FIRST + PACK * P], F32, name="old0"), keep.tile([P, P + T], F32, name="old1")]
-        w_raw = [
-            [keep.tile([P, PACK, P], F32, name="w_raw00")[:], old[0][:, FIRST:].rearrange("p (t m) -> p t m", t=PACK)],
-            [keep.tile([P, PACK, P], F32, name=f"w_raw1{z}")[:] for z in range(PASSES)],
-        ]
+        twin = keep.tile([P, U], F32, name="twin")
+        w_raw = [keep.tile([P, PACK, N], F32, name=f"w_raw{z}") for z in range(PASSES)]
+        w_bf = [keep.tile([P, N, PACK], BF16, name=f"w_bf{z}", align_bytes=64) for z in range(PASSES)]
+        w_codes = [keep.tile([P, N], U32, name=f"w_codes{z}", align_bytes=64) for z in range(PASSES)]
+        w_scale = [keep.tile([P, N], U8, name=f"w_scale{z}", align_bytes=64) for z in range(PASSES)]
+        x_parts = [(0, FIRST), (FIRST, T)]
+        x_codes = [keep.tile([P, PASSES, 2 * (hi - lo)], U8, name=f"x_codes{lo}", align_bytes=64) for lo, hi in x_parts]
+        x_scale = keep.tile([P, PASSES, T], U8, name="x_scale", align_bytes=64)
+        old = [keep.tile([P, T], F32, name=f"old{b}") for b in range(ROW_GROUPS)]
         new = [keep.tile([P, T], F32, name=f"new{b}") for b in range(ROW_GROUPS)]
-        acc = [[psum.tile([P, HALF], F32, name=f"acc{b}{h}") for h in range(HALVES)] for b in range(ROW_GROUPS)]
-        narrow_acc = [acc[0][0]] + [psum.tile([P, HALF], F32, name=f"narrow_acc{g}") for g in range(1, NARROW)]
 
-        def spare(name, tag=None):
-            return keep.tile([P, HALF], F32, name=name, tag=tag or name, align_bytes=64)
+        def load_w(z):
+            nc.sync.dma_start(w_raw[z][:], w1.rearrange("(z p t) m -> z p t m", p=P, t=PACK)[z])
 
-        w_view = w1.rearrange("(z p t) m -> z p t m", p=P, t=PACK)
-
-        def load_w(b, z):
-            nc.sync.dma_start(w_raw[b][z], w_view[z, :, :, b * P:(b + 1) * P])
-
-        def load_scales(h, queue):
+        def load_scales():
             for r in range(SCALE_ROWS):
-                queue.dma_start(
-                    x_scale[h][r:P:QUADRANT, :, :].bitcast(I32),
-                    x_scales.rearrange("z (q r) c -> r q z c", r=SCALE_ROWS)[r][:, :, h * HALF:(h + 1) * HALF].bitcast(I32),
+                nc.scalar.dma_start(
+                    x_scale[r:P:QUADRANT, :, :].bitcast(I32),
+                    x_scales.rearrange("z (q r) c -> r q z c", r=SCALE_ROWS)[r].bitcast(I32),
                 )
 
-        def load_x(h, z, lo=0, hi=HALF):
-            nc.sync.dma_start(x_codes[h][z][:, 2 * lo:2 * hi].bitcast(I32), x_words[z, :, 2 * (HALF * h + lo):2 * (HALF * h + hi)].bitcast(I32))
+        def load_x(part):
+            lo, hi = x_parts[part]
+            nc.sync.dma_start(x_codes[part][:].bitcast(I32), x_words.rearrange("z p c -> p z c")[:, :, 2 * lo:2 * hi].bitcast(I32))
 
-        def load_mem(b):
-            nc.sync.dma_start(window[b][:], mem[b * P:(b + 1) * P, :])
+        def load_mem(tile, b):
+            nc.sync.dma_start(tile[:], mem[b * P:(b + 1) * P, :])
 
-        def round_w(b, z, copy):
-            copy(w_bf[b][z][:].rearrange("p (c i) t -> p c t i", i=RUN), w_raw[b][z].rearrange("p t (c i) -> p c t i", i=RUN))
+        def round_w(copy, z, lo, hi):
+            copy(w_bf[z][:, lo:hi].rearrange("p (c i) t -> p c t i", i=RUN), w_raw[z][:, :, lo:hi].rearrange("p t (c i) -> p c t i", i=RUN))
 
-        def quantise(b, z):
-            nc.vector.quantize_mx(
-                out=w_codes[b][:, z:z + 1].rearrange("p z m -> p (z m)").bitcast(FP8X4),
-                scales=w_scale[b][:, z:z + 1].rearrange("p z m -> p (z m)"),
-                in_=w_bf[b][z][:].rearrange("p m t -> p (m t)"),
-            )
+        def quantise(z):
+            nc.vector.quantize_mx(out=w_codes[z][:].bitcast(FP8X4), scales=w_scale[z][:], in_=w_bf[z][:].rearrange("p m t -> p (m t)"))
 
-        def project(bank, b, h, z, lo, hi):
-            nc.tensor.matmul_mx(
-                out=bank[:, :hi - lo],
-                lhsT=w_codes[b][:, z, :].bitcast(FP8X4),
-                lhsT_scale=w_scale[b][:, z, :],
-                rhs=x_codes[h][z][:, 2 * lo:2 * hi].bitcast(FP4X4),
-                rhs_scale=x_scale[h][:, z, lo:hi],
-                start=(z == 0),
-                stop=(z == PASSES - 1),
-            )
+        def project(b, lo, *widths):
+            bank = psum.tile([P, HALF], F32, name=f"bank{b}_{lo}")
+            at = 0
+            for width in widths:
+                part = 0 if lo + at < FIRST else 1
+                first = lo + at - x_parts[part][0]
+                for z in range(PASSES):
+                    nc.tensor.matmul_mx(
+                        out=bank[:, at:at + width],
+                        lhsT=w_codes[z][:, b * P:(b + 1) * P].bitcast(FP8X4),
+                        lhsT_scale=w_scale[z][:, b * P:(b + 1) * P],
+                        rhs=x_codes[part][:, z, 2 * first:2 * (first + width)].bitcast(FP4X4),
+                        rhs_scale=x_scale[:, z, lo + at:lo + at + width],
+                        start=(z == 0),
+                        stop=(z == PASSES - 1),
+                    )
+                at += width
+            return bank
 
-        def listed(b, lo, hi):
-            return window[b][:].indirect(offsets[:, lo // STRIPE:hi // STRIPE])
+        def listed(tile, lo, hi):
+            return tile[:].indirect(offsets[:, lo // STRIPE:hi // STRIPE])
 
-        def gather(b, lo, hi):
-            nc.vector.tensor_copy(old[b][:, lo:hi], listed(b, lo, hi))
+        def scalar_copy(to, source):
+            nc.scalar.activation(to, source, COPY)
 
-        def larger(bank, b, lo, hi):
-            nc.vector.tensor_tensor(new[b][:, lo:hi], bank[:, :hi - lo], old[b][:, lo:hi], MAX)
+        def gather(copy, b, lo, hi):
+            copy(old[b][:, lo:hi], listed(window[b], lo, hi))
 
-        def scatter(b, lo, hi):
-            nc.vector.tensor_copy(listed(b, lo, hi), new[b][:, lo:hi])
+        def larger(b, lo, hi, sums):
+            nc.vector.tensor_tensor(new[b][:, lo:hi], sums, old[b][:, lo:hi], MAX)
 
-        def store(b):
-            nc.sync.dma_start(out[b * P:(b + 1) * P, :], window[b][:])
+        def scatter(copy, tile, b, lo, hi):
+            copy(listed(tile, lo, hi), new[b][:, lo:hi])
 
-        load_scales(0, nc.scalar)
-        load_w(0, 0)
+        load_scales()
+        for z in range(PASSES):
+            load_w(z)
         nc.sync.dma_start(offsets[:], slot)
-        load_mem(0)
-        load_w(0, 1)
-        for z in range(PASSES):
-            load_x(0, z)
-        load_w(1, 0)
-        load_scales(1, nc.sync)
-        load_x(1, 0)
-        load_x(1, 1, 0, HALF // 2)
-        load_w(1, 1)
-        load_mem(1)
-        load_x(1, 1, HALF // 2, HALF)
+        load_mem(window[0], 0)
+        load_x(0)
+        load_x(1)
+        load_mem(window[1], 1)
+        load_mem(twin, 1)
 
-        round_w(0, 0, nc.vector.tensor_copy)
-        quantise(0, 0)
-        rounded = w_bf[0][1][:].rearrange("p (c i) t -> p c t i", i=RUN)
-        staged = w_raw[0][1].rearrange("p t (c i) -> p c t i", i=RUN)
-        share = 3 * P // (4 * RUN)
-        nc.scalar.copy(rounded[:, :share], staged[:, :share])
-        nc.gpsimd.tensor_scalar(rounded[:, share:], staged[:, share:], 1.0, 0.0, mybir.AluOpType.mult, mybir.AluOpType.add)
-        gather(0, 0, FIRST)
-        quantise(0, 1)
-        gather(0, FIRST, T)
         for z in range(PASSES):
-            for g in range(NARROW):
-                project(narrow_acc[g], 0, 0, z, g * P, (g + 1) * P)
-        for z in range(PASSES):
-            round_w(1, z, nc.scalar.copy)
-        project(acc[0][1], 0, 1, 0, 0, HALF)
-        for g in range(NARROW):
-            larger(narrow_acc[g], 0, g * P, (g + 1) * P)
-        quantise(1, 0)
-        scatter(0, 0, EARLY)
-        quantise(1, 1)
-        for z in range(PASSES):
-            project(acc[1][0], 1, 0, z, 0, HALF)
-            project(narrow_acc[0], 1, 1, z, 0, P)
-        for g in reversed(range(1, NARROW)):
-            for z in range(PASSES):
-                project(acc[1][1][:, (g - 1) * P:], 1, 1, z, g * P, (g + 1) * P)
-        project(acc[0][1], 0, 1, 1, 0, HALF)
+            round_w(nc.vector.tensor_copy, z, 0, ROUND_SPLIT)
+            round_w(nc.scalar.copy, z, ROUND_SPLIT, N)
+            quantise(z)
 
-        gather(1, MASKED, T)
-        gather(1, 0, MASKED)
-        larger(acc[1][1], 1, MASKED, T)
-        larger(acc[0][1], 0, HALF, T)
-        scatter(1, MASKED, T)
-        scatter(0, EARLY, T)
-        store(0)
+        gather(nc.vector.tensor_copy, 0, 0, FIRST)
+        gather(nc.vector.tensor_copy, 0, FIRST, VECTOR_FIRST)
+        gather(scalar_copy, 0, VECTOR_FIRST, T)
+        larger(0, 0, FIRST, project(0, 0, FIRST)[:, :FIRST])
+        scatter(scalar_copy, window[0], 0, 0, FIRST)
+        for lo in range(FIRST, T, PIECE):
+            larger(0, lo, lo + PIECE, project(0, lo, 2 * P, P)[:, :PIECE])
+            scatter(scalar_copy, window[0], 0, lo, lo + PIECE)
+        nc.sync.dma_start(out[:P, :], window[0][:])
 
-        both, mask, part = [keep.tile([P, 2, MASKED], F32, name=name) for name in ("both", "mask", "part")]
-        gap, sign = [keep.tile([P, MASKED], F32, name=name) for name in ("gap", "sign")]
-        pieces = [slice(0, 2 * P), slice(2 * P, MASKED)]
-        nc.scalar.copy(both[:, 1, :HALF], acc[1][0][:])
-        nc.scalar.copy(both[:, 1, HALF:], narrow_acc[0][:, :P])
-        for c in pieces:
-            nc.gpsimd.tensor_tensor(gap[:, c], old[1][:, c], both[:, 1, c], ALU.subtract)
-        nc.gpsimd.tensor_scalar(both[:, 0, :], old[1][:, :MASKED], float("inf"), LOWEST, ALU.min, ALU.max)
-        for c in pieces:
-            nc.scalar.activation(sign[:, c], gap[:, c], ACT.Sign)
-            nc.scalar.activation(mask[:, 0, c], sign[:, c], ACT.Copy, bias=0.5, scale=0.5)
-            nc.scalar.activation(mask[:, 1, c], sign[:, c], ACT.Copy, bias=0.5, scale=-0.5)
-            nc.gpsimd.tensor_tensor(part[:, :, c], both[:, :, c], mask[:, :, c], ALU.mult)
-        nc.vector.tensor_tensor(listed(1, 0, MASKED), part[:, 0, :], part[:, 1, :], ALU.add)
-        store(1)
+        gather(nc.vector.tensor_copy, 1, 0, HALF)
+        gather(nc.vector.tensor_copy, 1, HALF, T)
+        larger(1, 0, HALF, project(1, 0, FIRST, HALF - FIRST)[:])
+        upper = project(1, HALF, HALF)
+        larger(1, HALF, SPLIT, upper[:, :SPLIT - HALF])
+        larger(1, SPLIT, T, upper[:, SPLIT - HALF:])
+        scatter(nc.vector.tensor_copy, window[1], 1, 0, SPLIT)
+        scatter(scalar_copy, twin, 1, SPLIT, T)
+        lo = 0
+        for width in MERGE:
+            columns = slice(lo, lo + width)
+            nc.vector.tensor_tensor(window[1][:, columns], window[1][:, columns], twin[:, columns], MAX)
+            nc.sync.dma_start(out[P:, columns], window[1][:, columns])
+            lo += width

@@ -28,9 +28,9 @@ SCALE_ROWS = 4
 RUN = 4
 FIRST = 256
 PIECE = 384
-VECTOR_FIRST = 480
-ROUND_SPLIT = 192
-SPLIT = 672
+VECTOR_FIRST = 448
+ROUND_SPLIT = 96
+SPLIT = 640
 MERGE = [512, 512, 512, 512]
 
 
@@ -43,18 +43,18 @@ def tile_picked_widxput_max_l_kernel(tc, x_words, x_scales, mem, w1, slot, out):
         offsets = keep.tile([P, T // STRIPE], U16, name="offsets")
         window = [keep.tile([P, U], F32, name=f"window{b}") for b in range(ROW_GROUPS)]
         twin = keep.tile([P, U], F32, name="twin")
-        w_raw = [keep.tile([P, PACK, N], F32, name=f"w_raw{z}") for z in range(PASSES)]
-        w_bf = [keep.tile([P, N, PACK], BF16, name=f"w_bf{z}", align_bytes=64) for z in range(PASSES)]
-        w_codes = [keep.tile([P, N], U32, name=f"w_codes{z}", align_bytes=64) for z in range(PASSES)]
-        w_scale = [keep.tile([P, N], U8, name=f"w_scale{z}", align_bytes=64) for z in range(PASSES)]
+        w_raw = [[keep.tile([P, PACK, P], F32, name=f"w_raw{b}{z}") for z in range(PASSES)] for b in range(ROW_GROUPS)]
+        w_bf = [[keep.tile([P, P, PACK], BF16, name=f"w_bf{b}{z}", align_bytes=64) for z in range(PASSES)] for b in range(ROW_GROUPS)]
+        w_codes = [[keep.tile([P, P], U32, name=f"w_codes{b}{z}", align_bytes=64) for z in range(PASSES)] for b in range(ROW_GROUPS)]
+        w_scale = [[keep.tile([P, P], U8, name=f"w_scale{b}{z}", align_bytes=64) for z in range(PASSES)] for b in range(ROW_GROUPS)]
         x_parts = [(0, FIRST), (FIRST, T)]
         x_codes = [keep.tile([P, PASSES, 2 * (hi - lo)], U8, name=f"x_codes{lo}", align_bytes=64) for lo, hi in x_parts]
         x_scale = keep.tile([P, PASSES, T], U8, name="x_scale", align_bytes=64)
         old = [keep.tile([P, T], F32, name=f"old{b}") for b in range(ROW_GROUPS)]
         new = [keep.tile([P, T], F32, name=f"new{b}") for b in range(ROW_GROUPS)]
 
-        def load_w(z):
-            nc.sync.dma_start(w_raw[z][:], w1.rearrange("(z p t) m -> z p t m", p=P, t=PACK)[z])
+        def load_w(b, z):
+            nc.sync.dma_start(w_raw[b][z][:], w1.rearrange("(z p t) m -> z p t m", p=P, t=PACK)[z, :, :, b * P:(b + 1) * P])
 
         def load_scales():
             for r in range(SCALE_ROWS):
@@ -70,11 +70,11 @@ def tile_picked_widxput_max_l_kernel(tc, x_words, x_scales, mem, w1, slot, out):
         def load_mem(tile, b):
             nc.sync.dma_start(tile[:], mem[b * P:(b + 1) * P, :])
 
-        def round_w(copy, z, lo, hi):
-            copy(w_bf[z][:, lo:hi].rearrange("p (c i) t -> p c t i", i=RUN), w_raw[z][:, :, lo:hi].rearrange("p t (c i) -> p c t i", i=RUN))
+        def round_w(copy, b, z, lo, hi):
+            copy(w_bf[b][z][:, lo:hi].rearrange("p (c i) t -> p c t i", i=RUN), w_raw[b][z][:, :, lo:hi].rearrange("p t (c i) -> p c t i", i=RUN))
 
-        def quantise(z):
-            nc.vector.quantize_mx(out=w_codes[z][:].bitcast(FP8X4), scales=w_scale[z][:], in_=w_bf[z][:].rearrange("p m t -> p (m t)"))
+        def quantise(b, z):
+            nc.vector.quantize_mx(out=w_codes[b][z][:].bitcast(FP8X4), scales=w_scale[b][z][:], in_=w_bf[b][z][:].rearrange("p m t -> p (m t)"))
 
         def project(b, lo, *widths):
             bank = psum.tile([P, HALF], F32, name=f"bank{b}_{lo}")
@@ -85,8 +85,8 @@ def tile_picked_widxput_max_l_kernel(tc, x_words, x_scales, mem, w1, slot, out):
                 for z in range(PASSES):
                     nc.tensor.matmul_mx(
                         out=bank[:, at:at + width],
-                        lhsT=w_codes[z][:, b * P:(b + 1) * P].bitcast(FP8X4),
-                        lhsT_scale=w_scale[z][:, b * P:(b + 1) * P],
+                        lhsT=w_codes[b][z][:].bitcast(FP8X4),
+                        lhsT_scale=w_scale[b][z][:],
                         rhs=x_codes[part][:, z, 2 * first:2 * (first + width)].bitcast(FP4X4),
                         rhs_scale=x_scale[:, z, lo + at:lo + at + width],
                         start=(z == 0),
@@ -112,18 +112,20 @@ def tile_picked_widxput_max_l_kernel(tc, x_words, x_scales, mem, w1, slot, out):
 
         load_scales()
         for z in range(PASSES):
-            load_w(z)
+            load_w(0, z)
         nc.sync.dma_start(offsets[:], slot)
         load_mem(window[0], 0)
         load_x(0)
         load_x(1)
+        for z in range(PASSES):
+            load_w(1, z)
         load_mem(window[1], 1)
         load_mem(twin, 1)
 
         for z in range(PASSES):
-            round_w(nc.vector.tensor_copy, z, 0, ROUND_SPLIT)
-            round_w(nc.scalar.copy, z, ROUND_SPLIT, N)
-            quantise(z)
+            round_w(nc.vector.tensor_copy, 0, z, 0, ROUND_SPLIT)
+            round_w(nc.scalar.copy, 0, z, ROUND_SPLIT, P)
+            quantise(0, z)
 
         gather(nc.vector.tensor_copy, 0, 0, FIRST)
         gather(nc.vector.tensor_copy, 0, FIRST, VECTOR_FIRST)
@@ -135,6 +137,9 @@ def tile_picked_widxput_max_l_kernel(tc, x_words, x_scales, mem, w1, slot, out):
             scatter(scalar_copy, window[0], 0, lo, lo + PIECE)
         nc.sync.dma_start(out[:P, :], window[0][:])
 
+        for z in range(PASSES):
+            round_w(nc.vector.tensor_copy, 1, z, 0, P)
+            quantise(1, z)
         gather(nc.vector.tensor_copy, 1, 0, HALF)
         gather(nc.vector.tensor_copy, 1, HALF, T)
         larger(1, 0, HALF, project(1, 0, FIRST, HALF - FIRST)[:])

@@ -31,6 +31,7 @@ PIECE = 384
 VECTOR_FIRST = 448
 ROUND_SPLIT = 96
 SPLIT = 640
+FILL = 128
 MERGE = [512, 512, 512, 512]
 
 
@@ -47,7 +48,7 @@ def tile_picked_widxput_max_l_kernel(tc, x_words, x_scales, mem, w1, slot, out):
         w_bf = [[keep.tile([P, P, PACK], BF16, name=f"w_bf{b}{z}", align_bytes=64) for z in range(PASSES)] for b in range(ROW_GROUPS)]
         w_codes = [[keep.tile([P, P], U32, name=f"w_codes{b}{z}", align_bytes=64) for z in range(PASSES)] for b in range(ROW_GROUPS)]
         w_scale = [[keep.tile([P, P], U8, name=f"w_scale{b}{z}", align_bytes=64) for z in range(PASSES)] for b in range(ROW_GROUPS)]
-        x_parts = [(0, FIRST), (FIRST, T)]
+        x_parts = [(0, FIRST), (FIRST, FIRST + PIECE), (FIRST + PIECE, T)]
         x_codes = [keep.tile([P, PASSES, 2 * (hi - lo)], U8, name=f"x_codes{lo}", align_bytes=64) for lo, hi in x_parts]
         x_scale = keep.tile([P, PASSES, T], U8, name="x_scale", align_bytes=64)
         old = [keep.tile([P, T], F32, name=f"old{b}") for b in range(ROW_GROUPS)]
@@ -76,23 +77,23 @@ def tile_picked_widxput_max_l_kernel(tc, x_words, x_scales, mem, w1, slot, out):
         def quantise(b, z):
             nc.vector.quantize_mx(out=w_codes[b][z][:].bitcast(FP8X4), scales=w_scale[b][z][:], in_=w_bf[b][z][:].rearrange("p m t -> p (m t)"))
 
-        def project(b, lo, *widths):
-            bank = psum.tile([P, HALF], F32, name=f"bank{b}_{lo}")
+        def project(b, *spans):
+            bank = psum.tile([P, HALF], F32, name=f"bank{b}_{spans[0][0]}")
             at = 0
-            for width in widths:
-                part = 0 if lo + at < FIRST else 1
-                first = lo + at - x_parts[part][0]
+            for lo, hi in spans:
+                part = [lo < end for begin, end in x_parts].index(True)
+                first = lo - x_parts[part][0]
                 for z in range(PASSES):
                     nc.tensor.matmul_mx(
-                        out=bank[:, at:at + width],
+                        out=bank[:, at:at + hi - lo],
                         lhsT=w_codes[b][z][:].bitcast(FP8X4),
                         lhsT_scale=w_scale[b][z][:],
-                        rhs=x_codes[part][:, z, 2 * first:2 * (first + width)].bitcast(FP4X4),
-                        rhs_scale=x_scale[:, z, lo + at:lo + at + width],
+                        rhs=x_codes[part][:, z, 2 * first:2 * (first + hi - lo)].bitcast(FP4X4),
+                        rhs_scale=x_scale[:, z, lo:hi],
                         start=(z == 0),
                         stop=(z == PASSES - 1),
                     )
-                at += width
+                at += hi - lo
             return bank
 
         def listed(tile, lo, hi):
@@ -120,6 +121,7 @@ def tile_picked_widxput_max_l_kernel(tc, x_words, x_scales, mem, w1, slot, out):
         for z in range(PASSES):
             load_w(1, z)
         load_mem(window[1], 1)
+        load_x(2)
         load_mem(twin, 1)
 
         for z in range(PASSES):
@@ -130,10 +132,10 @@ def tile_picked_widxput_max_l_kernel(tc, x_words, x_scales, mem, w1, slot, out):
         gather(nc.vector.tensor_copy, 0, 0, FIRST)
         gather(nc.vector.tensor_copy, 0, FIRST, VECTOR_FIRST)
         gather(scalar_copy, 0, VECTOR_FIRST, T)
-        larger(0, 0, FIRST, project(0, 0, FIRST)[:, :FIRST])
+        larger(0, 0, FIRST, project(0, (0, FIRST))[:, :FIRST])
         scatter(scalar_copy, window[0], 0, 0, FIRST)
         for lo in range(FIRST, T, PIECE):
-            larger(0, lo, lo + PIECE, project(0, lo, 2 * P, P)[:, :PIECE])
+            larger(0, lo, lo + PIECE, project(0, (lo, lo + 2 * P), (lo + 2 * P, lo + PIECE))[:, :PIECE])
             scatter(scalar_copy, window[0], 0, lo, lo + PIECE)
         nc.sync.dma_start(out[:P, :], window[0][:])
 
@@ -141,11 +143,13 @@ def tile_picked_widxput_max_l_kernel(tc, x_words, x_scales, mem, w1, slot, out):
             round_w(nc.vector.tensor_copy, 1, z, 0, P)
             quantise(1, z)
         gather(nc.vector.tensor_copy, 1, 0, HALF)
-        gather(nc.vector.tensor_copy, 1, HALF, T)
-        larger(1, 0, HALF, project(1, 0, FIRST, HALF - FIRST)[:])
-        upper = project(1, HALF, HALF)
-        larger(1, HALF, SPLIT, upper[:, :SPLIT - HALF])
-        larger(1, SPLIT, T, upper[:, SPLIT - HALF:])
+        gather(nc.vector.tensor_copy, 1, HALF, T - FILL)
+        gather(scalar_copy, 1, T - FILL, T)
+        ends = project(1, (0, FIRST), (FIRST, PIECE), (T - P, T))
+        middle = project(1, (PIECE, FIRST + PIECE), (FIRST + PIECE, T - P))
+        larger(1, 0, PIECE, ends[:, :PIECE])
+        larger(1, PIECE, T - P, middle[:])
+        larger(1, T - P, T, ends[:, PIECE:])
         scatter(nc.vector.tensor_copy, window[1], 1, 0, SPLIT)
         scatter(scalar_copy, twin, 1, SPLIT, T)
         lo = 0

@@ -30,8 +30,8 @@ FIRST = 256
 PIECE = 384
 VECTOR_FIRST = 448
 ROUND_SPLIT = 96
-SPLIT = 640
-FILL = 128
+SPLIT = 384
+FILL = 192
 MERGE = [512, 512, 512, 512]
 
 
@@ -142,16 +142,15 @@ def tile_picked_widxput_max_l_kernel(tc, x_words, x_scales, mem, w1, slot, out):
         for z in range(PASSES):
             round_w(nc.vector.tensor_copy, 1, z, 0, P)
             quantise(1, z)
-        gather(nc.vector.tensor_copy, 1, 0, HALF)
-        gather(nc.vector.tensor_copy, 1, HALF, T - FILL)
-        gather(scalar_copy, 1, T - FILL, T)
+        gather(nc.vector.tensor_copy, 1, FILL, T)
+        gather(scalar_copy, 1, 0, FILL)
         ends = project(1, (0, FIRST), (FIRST, PIECE), (T - P, T))
         middle = project(1, (PIECE, FIRST + PIECE), (FIRST + PIECE, T - P))
-        larger(1, 0, PIECE, ends[:, :PIECE])
         larger(1, PIECE, T - P, middle[:])
         larger(1, T - P, T, ends[:, PIECE:])
-        scatter(nc.vector.tensor_copy, window[1], 1, 0, SPLIT)
-        scatter(scalar_copy, twin, 1, SPLIT, T)
+        larger(1, 0, PIECE, ends[:, :PIECE])
+        scatter(nc.vector.tensor_copy, window[1], 1, SPLIT, T)
+        scatter(scalar_copy, twin, 1, 0, SPLIT)
         lo = 0
         for width in MERGE:
             columns = slice(lo, lo + width)

@@ -50,18 +50,20 @@ def tile_picked_widxput_max_l_kernel(tc, x_words, x_scales, mem, w1, slot, out):
         w_scale = [[keep.tile([P, P], U8, name=f"w_scale{b}{z}", align_bytes=64) for z in range(PASSES)] for b in range(ROW_GROUPS)]
         x_parts = [(0, FIRST), (FIRST, FIRST + PIECE), (FIRST + PIECE, T)]
         x_codes = [keep.tile([P, PASSES, 2 * (hi - lo)], U8, name=f"x_codes{lo}", align_bytes=64) for lo, hi in x_parts]
-        x_scale = keep.tile([P, PASSES, T], U8, name="x_scale", align_bytes=64)
+        scale_parts = [(0, FIRST + PIECE), (FIRST + PIECE, T)]
+        x_scale = [keep.tile([P, PASSES, hi - lo], U8, name=f"x_scale{lo}", align_bytes=64) for lo, hi in scale_parts]
         old = [keep.tile([P, T], F32, name=f"old{b}") for b in range(ROW_GROUPS)]
         new = [keep.tile([P, T], F32, name=f"new{b}") for b in range(ROW_GROUPS)]
 
         def load_w(b, z):
             nc.sync.dma_start(w_raw[b][z][:], w1.rearrange("(z p t) m -> z p t m", p=P, t=PACK)[z, :, :, b * P:(b + 1) * P])
 
-        def load_scales():
+        def load_scales(queue, part):
+            lo, hi = scale_parts[part]
             for r in range(SCALE_ROWS):
-                nc.scalar.dma_start(
-                    x_scale[r:P:QUADRANT, :, :].bitcast(I32),
-                    x_scales.rearrange("z (q r) c -> r q z c", r=SCALE_ROWS)[r].bitcast(I32),
+                queue.dma_start(
+                    x_scale[part][r:P:QUADRANT, :, :].bitcast(I32),
+                    x_scales.rearrange("z (q r) c -> r q z c", r=SCALE_ROWS)[r][:, :, lo:hi].bitcast(I32),
                 )
 
         def load_x(part):
@@ -89,7 +91,7 @@ def tile_picked_widxput_max_l_kernel(tc, x_words, x_scales, mem, w1, slot, out):
                         lhsT=w_codes[b][z][:].bitcast(FP8X4),
                         lhsT_scale=w_scale[b][z][:],
                         rhs=x_codes[part][:, z, 2 * first:2 * (first + hi - lo)].bitcast(FP4X4),
-                        rhs_scale=x_scale[:, z, lo:hi],
+                        rhs_scale=x_scale[part // 2][:, z, lo - scale_parts[part // 2][0]:hi - scale_parts[part // 2][0]],
                         start=(z == 0),
                         stop=(z == PASSES - 1),
                     )
@@ -111,17 +113,18 @@ def tile_picked_widxput_max_l_kernel(tc, x_words, x_scales, mem, w1, slot, out):
         def scatter(copy, tile, b, lo, hi):
             copy(listed(tile, lo, hi), new[b][:, lo:hi])
 
-        load_scales()
+        load_scales(nc.scalar, 0)
         for z in range(PASSES):
             load_w(0, z)
-        nc.sync.dma_start(offsets[:], slot)
-        load_mem(window[0], 0)
         load_x(0)
+        load_mem(window[0], 0)
+        nc.sync.dma_start(offsets[:], slot)
         load_x(1)
         for z in range(PASSES):
             load_w(1, z)
         load_mem(window[1], 1)
         load_x(2)
+        load_scales(nc.sync, 1)
         load_mem(twin, 1)
 
         for z in range(PASSES):
@@ -144,8 +147,8 @@ def tile_picked_widxput_max_l_kernel(tc, x_words, x_scales, mem, w1, slot, out):
             quantise(1, z)
         gather(nc.vector.tensor_copy, 1, FILL, T)
         gather(scalar_copy, 1, 0, FILL)
-        ends = project(1, (0, FIRST), (FIRST, PIECE), (T - P, T))
         middle = project(1, (PIECE, FIRST + PIECE), (FIRST + PIECE, T - P))
+        ends = project(1, (0, FIRST), (FIRST, PIECE), (T - P, T))
         larger(1, PIECE, T - P, middle[:])
         larger(1, T - P, T, ends[:, PIECE:])
         larger(1, 0, PIECE, ends[:, :PIECE])

@@ -31,7 +31,7 @@ PIECE = 384
 VECTOR_FIRST = 448
 ROUND_SPLIT = 96
 SPLIT = 384
-FILL = 192
+FILL = 224
 MERGE = [512, 512, 512, 512]
 
 
@@ -116,9 +116,9 @@ def tile_picked_widxput_max_l_kernel(tc, x_words, x_scales, mem, w1, slot, out):
         load_scales(nc.scalar, 0)
         for z in range(PASSES):
             load_w(0, z)
-        load_x(0)
-        load_mem(window[0], 0)
         nc.sync.dma_start(offsets[:], slot)
+        load_mem(window[0], 0)
+        load_x(0)
         load_x(1)
         for z in range(PASSES):
             load_w(1, z)
@@ -135,7 +135,8 @@ def tile_picked_widxput_max_l_kernel(tc, x_words, x_scales, mem, w1, slot, out):
         gather(nc.vector.tensor_copy, 0, 0, FIRST)
         gather(nc.vector.tensor_copy, 0, FIRST, VECTOR_FIRST)
         gather(scalar_copy, 0, VECTOR_FIRST, T)
-        larger(0, 0, FIRST, project(0, (0, FIRST))[:, :FIRST])
+        for lo in range(0, FIRST, P):
+            larger(0, lo, lo + P, project(0, (lo, lo + P))[:, :P])
         scatter(scalar_copy, window[0], 0, 0, FIRST)
         for lo in range(FIRST, T, PIECE):
             larger(0, lo, lo + PIECE, project(0, (lo, lo + 2 * P), (lo + 2 * P, lo + PIECE))[:, :PIECE])

@@ -32,7 +32,7 @@ VECTOR_FIRST = 448
 ROUND_SPLIT = 96
 SPLIT = 384
 FILL = 224
-MERGE = [512, 512, 512, 512]
+MERGE = [384, 512, 576, 576]
 
 
 def tile_picked_widxput_max_l_kernel(tc, x_words, x_scales, mem, w1, slot, out):

@@ -28,7 +28,7 @@ SCALE_ROWS = 4
 RUN = 4
 FIRST = 256
 PIECE = 384
-VECTOR_FIRST = 448
+VECTOR_FIRST = 416
 ROUND_SPLIT = 96
 SPLIT = 384
 FILL = 224
@@ -66,9 +66,9 @@ def tile_picked_widxput_max_l_kernel(tc, x_words, x_scales, mem, w1, slot, out):
                     x_scales.rearrange("z (q r) c -> r q z c", r=SCALE_ROWS)[r][:, :, lo:hi].bitcast(I32),
                 )
 
-        def load_x(part):
+        def load_x(part, begin=0, end=PASSES):
             lo, hi = x_parts[part]
-            nc.sync.dma_start(x_codes[part][:].bitcast(I32), x_words.rearrange("z p c -> p z c")[:, :, 2 * lo:2 * hi].bitcast(I32))
+            nc.sync.dma_start(x_codes[part][:, begin:end].bitcast(I32), x_words.rearrange("z p c -> p z c")[:, begin:end, 2 * lo:2 * hi].bitcast(I32))
 
         def load_mem(tile, b):
             nc.sync.dma_start(tile[:], mem[b * P:(b + 1) * P, :])
@@ -116,9 +116,10 @@ def tile_picked_widxput_max_l_kernel(tc, x_words, x_scales, mem, w1, slot, out):
         load_scales(nc.scalar, 0)
         for z in range(PASSES):
             load_w(0, z)
-        nc.sync.dma_start(offsets[:], slot)
+        load_x(0, 0, 1)
         load_mem(window[0], 0)
-        load_x(0)
+        nc.sync.dma_start(offsets[:], slot)
+        load_x(0, 1, PASSES)
         load_x(1)
         for z in range(PASSES):
             load_w(1, z)
@@ -135,13 +136,13 @@ def tile_picked_widxput_max_l_kernel(tc, x_words, x_scales, mem, w1, slot, out):
         gather(nc.vector.tensor_copy, 0, 0, FIRST)
         gather(nc.vector.tensor_copy, 0, FIRST, VECTOR_FIRST)
         gather(scalar_copy, 0, VECTOR_FIRST, T)
-        for lo in range(0, FIRST, P):
-            larger(0, lo, lo + P, project(0, (lo, lo + P))[:, :P])
+        larger(0, 0, FIRST, project(0, (0, FIRST))[:, :FIRST])
         scatter(scalar_copy, window[0], 0, 0, FIRST)
         for lo in range(FIRST, T, PIECE):
             larger(0, lo, lo + PIECE, project(0, (lo, lo + 2 * P), (lo + 2 * P, lo + PIECE))[:, :PIECE])
             scatter(scalar_copy, window[0], 0, lo, lo + PIECE)
-        nc.sync.dma_start(out[:P, :], window[0][:])
+        for lo in range(0, U, FIRST):
+            nc.sync.dma_start(out[:P, lo:lo + FIRST], window[0][:, lo:lo + FIRST])
 
         for z in range(PASSES):
             round_w(nc.vector.tensor_copy, 1, z, 0, P)

from contextlib import ExitStack

import concourse.mybir as mybir

K, T, N, U = 1024, 1024, 256, 2048
FLOPS = 2 * K * T * N

F32 = mybir.dt.float32
BF16 = mybir.dt.bfloat16
I32 = mybir.dt.int32
U32 = mybir.dt.uint32
U16 = mybir.dt.uint16
U8 = mybir.dt.uint8
FP8X4 = mybir.dt.float8_e4m3fn_x4
FP4X4 = mybir.dt.float4_e2m1fn_x4
MAX = mybir.AluOpType.max
COPY = mybir.ActivationFunctionType.Copy

P = 128
PACK = 4
PASSES = K // (P * PACK)
ROW_GROUPS = N // P
HALF = 512
HALVES = T // HALF
STRIPE = 16
QUADRANT = 32
SCALE_ROWS = 4
RUN = 4
FIRST = 256
PIECE = 384
VECTOR_FIRST = 416
ROUND_SPLIT = 96
SPLIT = 384
FILL = 224
MERGE = [384, 512, 576, 576]


def tile_picked_widxput_max_l_kernel(tc, x_words, x_scales, mem, w1, slot, out):
    nc = tc.nc
    with ExitStack() as ctx:
        keep = ctx.enter_context(tc.tile_pool(name="keep", bufs=1))
        psum = ctx.enter_context(tc.psum_pool(name="psum", bufs=1))

        offsets = keep.tile([P, T // STRIPE], U16, name="offsets")
        window = [keep.tile([P, U], F32, name=f"window{b}") for b in range(ROW_GROUPS)]
        twin = keep.tile([P, U], F32, name="twin")
        w_raw = [[keep.tile([P, PACK, P], F32, name=f"w_raw{b}{z}") for z in range(PASSES)] for b in range(ROW_GROUPS)]
        w_bf = [[keep.tile([P, P, PACK], BF16, name=f"w_bf{b}{z}", align_bytes=64) for z in range(PASSES)] for b in range(ROW_GROUPS)]
        w_codes = [[keep.tile([P, P], U32, name=f"w_codes{b}{z}", align_bytes=64) for z in range(PASSES)] for b in range(ROW_GROUPS)]
        w_scale = [[keep.tile([P, P], U8, name=f"w_scale{b}{z}", align_bytes=64) for z in range(PASSES)] for b in range(ROW_GROUPS)]
        x_parts = [(0, FIRST), (FIRST, FIRST + PIECE), (FIRST + PIECE, T)]
        x_codes = [keep.tile([P, PASSES, 2 * (hi - lo)], U8, name=f"x_codes{lo}", align_bytes=64) for lo, hi in x_parts]
        scale_parts = [(0, FIRST + PIECE), (FIRST + PIECE, T)]
        x_scale = [keep.tile([P, PASSES, hi - lo], U8, name=f"x_scale{lo}", align_bytes=64) for lo, hi in scale_parts]
        old = [keep.tile([P, T], F32, name=f"old{b}") for b in range(ROW_GROUPS)]
        new = [keep.tile([P, T], F32, name=f"new{b}") for b in range(ROW_GROUPS)]

        def load_w(b, z):
            nc.sync.dma_start(w_raw[b][z][:], w1.rearrange("(z p t) m -> z p t m", p=P, t=PACK)[z, :, :, b * P:(b + 1) * P])

        def load_scales(queue, part):
            lo, hi = scale_parts[part]
            for r in range(SCALE_ROWS):
                queue.dma_start(
                    x_scale[part][r:P:QUADRANT, :, :].bitcast(I32),
                    x_scales.rearrange("z (q r) c -> r q z c", r=SCALE_ROWS)[r][:, :, lo:hi].bitcast(I32),
                )

        def load_x(part, begin=0, end=PASSES):
            lo, hi = x_parts[part]
            nc.sync.dma_start(x_codes[part][:, begin:end].bitcast(I32), x_words.rearrange("z p c -> p z c")[:, begin:end, 2 * lo:2 * hi].bitcast(I32))

        def load_mem(tile, b):
            nc.sync.dma_start(tile[:], mem[b * P:(b + 1) * P, :])

        def round_w(copy, b, z, lo, hi):
            copy(w_bf[b][z][:, lo:hi].rearrange("p (c i) t -> p c t i", i=RUN), w_raw[b][z][:, :, lo:hi].rearrange("p t (c i) -> p c t i", i=RUN))

        def quantise(b, z):
            nc.vector.quantize_mx(out=w_codes[b][z][:].bitcast(FP8X4), scales=w_scale[b][z][:], in_=w_bf[b][z][:].rearrange("p m t -> p (m t)"))

        def project(b, *spans):
            bank = psum.tile([P, HALF], F32, name=f"bank{b}_{spans[0][0]}")
            at = 0
            for lo, hi in spans:
                part = [lo < end for begin, end in x_parts].index(True)
                first = lo - x_parts[part][0]
                for z in range(PASSES):
                    nc.tensor.matmul_mx(
                        out=bank[:, at:at + hi - lo],
                        lhsT=w_codes[b][z][:].bitcast(FP8X4),
                        lhsT_scale=w_scale[b][z][:],
                        rhs=x_codes[part][:, z, 2 * first:2 * (first + hi - lo)].bitcast(FP4X4),
                        rhs_scale=x_scale[part // 2][:, z, lo - scale_parts[part // 2][0]:hi - scale_parts[part // 2][0]],
                        start=(z == 0),
                        stop=(z == PASSES - 1),
                    )
                at += hi - lo
            return bank

        def listed(tile, lo, hi):
            return tile[:].indirect(offsets[:, lo // STRIPE:hi // STRIPE])

        def scalar_copy(to, source):
            nc.scalar.activation(to, source, COPY)

        def gather(copy, b, lo, hi):
            copy(old[b][:, lo:hi], listed(window[b], lo, hi))

        def larger(b, lo, hi, sums):
            nc.vector.tensor_tensor(new[b][:, lo:hi], sums, old[b][:, lo:hi], MAX)

        def scatter(copy, tile, b, lo, hi):
            copy(listed(tile, lo, hi), new[b][:, lo:hi])

        load_scales(nc.scalar, 0)
        for z in range(PASSES):
            load_w(0, z)
        load_x(0, 0, 1)
        load_mem(window[0], 0)
        nc.sync.dma_start(offsets[:], slot)
        load_x(0, 1, PASSES)
        load_x(1)
        for z in range(PASSES):
            load_w(1, z)
        load_mem(window[1], 1)
        load_x(2)
        load_scales(nc.sync, 1)
        load_mem(twin, 1)

        for z in range(PASSES):
            round_w(nc.vector.tensor_copy, 0, z, 0, ROUND_SPLIT)
            round_w(nc.scalar.copy, 0, z, ROUND_SPLIT, P)
            quantise(0, z)

        gather(nc.vector.tensor_copy, 0, 0, FIRST)
        gather(nc.vector.tensor_copy, 0, FIRST, VECTOR_FIRST)
        gather(scalar_copy, 0, VECTOR_FIRST, T)
        larger(0, 0, FIRST, project(0, (0, FIRST))[:, :FIRST])
        scatter(scalar_copy, window[0], 0, 0, FIRST)
        for lo in range(FIRST, T, PIECE):
            larger(0, lo, lo + PIECE, project(0, (lo, lo + 2 * P), (lo + 2 * P, lo + PIECE))[:, :PIECE])
            scatter(scalar_copy, window[0], 0, lo, lo + PIECE)
        for lo in range(0, U, FIRST):
            nc.sync.dma_start(out[:P, lo:lo + FIRST], window[0][:, lo:lo + FIRST])

        for z in range(PASSES):
            round_w(nc.vector.tensor_copy, 1, z, 0, P)
            quantise(1, z)
        gather(nc.vector.tensor_copy, 1, FILL, T)
        gather(scalar_copy, 1, 0, FILL)
        middle = project(1, (PIECE, FIRST + PIECE), (FIRST + PIECE, T - P))
        ends = project(1, (0, FIRST), (FIRST, PIECE), (T - P, T))
        larger(1, PIECE, T - P, middle[:])
        larger(1, T - P, T, ends[:, PIECE:])
        larger(1, 0, PIECE, ends[:, :PIECE])
        scatter(nc.vector.tensor_copy, window[1], 1, SPLIT, T)
        scatter(scalar_copy, twin, 1, 0, SPLIT)
        lo = 0
        for width in MERGE:
            columns = slice(lo, lo + width)
            nc.vector.tensor_tensor(window[1][:, columns], window[1][:, columns], twin[:, columns], MAX)
            nc.sync.dma_start(out[P:, columns], window[1][:, columns])
            lo += width
